import numpy as np
import ml_dtypes


def mxq(x, axis, fmt="e4m3"):
    dtype, down = {"e4m3": (ml_dtypes.float8_e4m3fn, 7), "e5m2": (ml_dtypes.float8_e5m2, 14)}[fmt]
    v = np.moveaxis(np.asarray(x, np.float32).astype(ml_dtypes.bfloat16).astype(np.float64), axis, -1)
    blocks = v.reshape(v.shape[:-1] + (-1, 32))
    amax = np.abs(blocks).max(-1, keepdims=True)
    byte = np.maximum(np.where(amax > 0, np.frexp(amax)[1] - 1 + 127, 0) - down, 1)
    scale = np.exp2(byte - 127.0)
    codes = (blocks / scale).astype(np.float32).astype(dtype).astype(np.float64)
    return np.moveaxis((codes * scale).reshape(v.shape), -1, axis)


WIDE = False


def mx_kscale(k):
    if not WIDE:
        return np.ones(k)
    levels = np.array([10, -10, 5, -5, 0])
    if k % 512:
        return np.exp2(np.random.permutation(np.resize(levels, k // 32))).repeat(32)
    a = np.empty((k // 512, 16))
    for p in range(k // 512):
        a[p, :8] = np.random.permutation(np.resize(levels, 8))
        for g in range(8):
            far = levels[np.abs(levels - a[p, g]) >= 10]
            a[p, g + 8] = far[np.random.randint(len(far))]
    return np.exp2(a.ravel()).repeat(32)


def f64(x):
    return np.asarray(x).astype(np.float64)


def striped(idx):
    return np.tile(idx.reshape(-1, 16).T, (8, 1)).astype(np.uint16)


def unstriped(offs):
    return offs[:16].T.reshape(-1).astype(np.int64)


def striped8(idx):
    return np.concatenate([x.reshape(-1, 16).T for x in idx]).astype(np.uint16)


def runs(offs, k):
    lists = np.stack([offs[16 * r : 16 * r + 16].T.reshape(-1) for r in range(8)]).astype(np.int64)
    return lists[np.arange(k) % 512 // 64]


def pack_weight(w):
    k, n = w.shape
    w = f64(np.asarray(w, np.float32).astype(ml_dtypes.bfloat16)).reshape(k // 32, 32, n)
    amax = np.abs(w).max(1)
    byte = np.clip(np.where(amax > 0, np.frexp(amax)[1] - 1 + 127 - 7, 1), 1, 254)
    scaled = (w * np.exp2(127.0 - byte)[:, None, :]).reshape(k, n).astype(np.float32)
    words = np.ascontiguousarray(scaled.reshape(k // 512, 128, 4, n).transpose(0, 1, 3, 2)).astype(ml_dtypes.float8_e4m3fn).view(np.uint8)
    return words, np.ascontiguousarray(byte.astype(np.uint8).reshape(k // 512, 16, n))


def unpack_weight(words, scales):
    g, p, n, _ = words.shape
    vals = np.ascontiguousarray(words).view(ml_dtypes.float8_e4m3fn).astype(np.float64) * np.repeat(np.exp2(scales.astype(np.float64) - 127.0), 8, axis=1)[..., None]
    return vals.transpose(0, 1, 3, 2).reshape(g * 512, n)


def sigmoid(v):
    return 1.0 / (1.0 + np.exp(-np.maximum(v, -700.0)))


K, T, S, V, H = 512, 2048, 512, 256, 512


def setup_inputs():
    n = np.random.standard_normal
    s = mx_kscale(K)[:, None]
    u = mx_kscale(S)
    packed_xT = pack_weight(n((K, T)) * s)
    return {
        "x_words": packed_xT[0],
        "x_scales": packed_xT[1],
        "w1": (n((K, H)) / np.sqrt(K) / s).astype(np.float32),
        "w2": (n((K, H)) / np.sqrt(K) / s).astype(np.float32),
        "sl": np.random.uniform(1.0, 2.0, (H, 1)).astype(np.float32),
        "th": (0.5 * n((H, 1))).astype(np.float32),
        "tau": np.random.uniform(0.2, 0.6, (H, 1)).astype(np.float32),
        "tau2": np.random.uniform(0.6, 1.0, (H, 1)).astype(np.float32),
        "ga": (np.random.uniform(0.5, 1.5, (H, 1)) * u[:, None]).astype(np.float32),
        "gb": (np.random.uniform(0.5, 1.5, (H, 1)) / u[:, None]).astype(np.float32),
        "tau3": np.random.uniform(0.3, 0.9, (S, 1)).astype(np.float32),
        "offs": striped8(np.random.randint(0, T, (8, S))),
        "two": striped(np.random.permutation(T)[:V]),
        "n1": striped8(np.stack([np.random.permutation(S) for _ in range(8)])),
        "n2": striped8(np.stack([np.random.permutation(S) for _ in range(8)])),
        "n3": striped8(np.stack([np.random.permutation(V) for _ in range(8)])),
        "n4": striped8(np.stack([np.random.permutation(V) for _ in range(8)])),
        "n5": striped8(np.stack([np.random.permutation(V) for _ in range(8)])),
        "n6": striped8(np.stack([np.random.permutation(V) for _ in range(8)])),
    }


def reference(x_words, x_scales, w1, w2, sl, th, tau, tau2, ga, gb, tau3, offs, two, n1, n2, n3, n4, n5, n6):
    xq = unpack_weight(x_words, x_scales)[np.arange(K)[:, None], runs(offs, K)]
    a = mxq(f64(w1), 0, "e4m3").T @ xq
    sg = sigmoid(f64(sl) * (a[np.arange(H)[:, None], runs(n1, H)] - f64(th)))
    st = a * sg
    z = f64(ga) * (st - (0.5 * (st[np.arange(H)[:, None], runs(n2, H)])))
    x_two = unpack_weight(x_words, x_scales)[:, unstriped(two)]
    b = mxq(f64(w2), 0, "e4m3").T @ x_two
    top = b.max(axis=1, keepdims=True)
    ea = np.exp(f64(tau) * (b[np.arange(H)[:, None], runs(n3, H)] - top))
    ea2 = np.exp(f64(tau2) * (b[np.arange(H)[:, None], runs(n4, H)] - top))
    z2 = f64(gb) * (3.0 * (ea - ea2))
    s = 0.0625 * ((mxq(z, 0, "e4m3").T @ mxq(z2, 0, "e4m3")))
    top2 = s.max(axis=1, keepdims=True)
    ea3 = np.exp(f64(tau3) * (s[np.arange(S)[:, None], runs(n5, S)] - top2))
    ea4 = np.exp(f64(tau3) * (s[np.arange(S)[:, None], runs(n6, S)] - top2))
    return s + np.log(ea3 + ea4 + 0.25)

@@ -1,0 +1,211 @@
+from contextlib import ExitStack
+
+import concourse.mybir as mybir
+
+K, T, S, V, H = 512, 2048, 512, 256, 512
+FLOPS = 2 * K * H * S + 2 * K * H * V + 2 * H * S * V
+
+F32 = mybir.dt.float32
+BF16 = mybir.dt.bfloat16
+I32 = mybir.dt.int32
+U32 = mybir.dt.uint32
+U16 = mybir.dt.uint16
+U8 = mybir.dt.uint8
+FP8X4 = mybir.dt.float8_e4m3fn_x4
+ALU = mybir.AluOpType
+ACT = mybir.ActivationFunctionType
+
+P = 128
+PACK = 4
+
+
+def tile_picked_hkqehpetwelg_none_p_kernel(tc, x_words, x_scales, w1, w2, sl, th, tau, tau2, ga, gb, tau3, offs, two, n1, n2, n3, n4, n5, n6, out):
+    nc = tc.nc
+    with ExitStack() as ctx:
+        keep = ctx.enter_context(tc.tile_pool(name="keep", bufs=1))
+        psum = ctx.enter_context(tc.psum_pool(name="psum", bufs=1))
+
+        def new(shape, dtype, name):
+            return keep.tile(shape, dtype, name=name, align_bytes=64)
+
+        def load_list(src, name):
+            t = new(list(src.shape), U16, name)
+            nc.sync.dma_start(t[:], src)
+            return t
+
+        def load_rows(src, name, queue):
+            t = new([P, PACK], F32, name)
+            queue.dma_start(out=t[:], in_=src.rearrange("(p t) o -> p (t o)", t=PACK))
+            return t
+
+        x_bytes = new([P, T], U8, "x_bytes")
+        nc.vector.memset(x_bytes[:].bitcast(I32), 0)
+        offs_sb = load_list(offs, "offs_sb")
+        scale_rows = x_scales[0].rearrange("(g r) c -> r g c", r=2)
+        for r in range(2):
+            nc.scalar.dma_start(out=x_bytes[r:P:16, :].bitcast(I32), in_=scale_rows[r].bitcast(I32))
+        two_sb = load_list(two, "two_sb")
+        x_sb = new([P, T], I32, "x_sb")
+        nc.sync.dma_start(out=x_sb[:], in_=x_words[0].rearrange("p c r -> p (c r)").bitcast(I32))
+        sl_sb = load_rows(sl, "sl_sb", nc.sync)
+        th_sb = load_rows(th, "th_sb", nc.sync)
+        n1_sb = load_list(n1, "n1_sb")
+        n2_sb = load_list(n2, "n2_sb")
+        n3_sb = load_list(n3, "n3_sb")
+        HALF = H // 2
+        w1_raw = [new([P, PACK, HALF], F32, "w1_raw%d" % h) for h in range(2)]
+        for h in range(2):
+            nc.sync.dma_start(out=w1_raw[h][:], in_=w1.rearrange("(p j) c -> p j c", j=PACK)[:, :, h * HALF : (h + 1) * HALF])
+        w2_raw = new([P, PACK, H], F32, "w2_raw")
+        nc.sync.dma_start(out=w2_raw[:], in_=w2.rearrange("(p j) c -> p j c", j=PACK))
+        n4_sb = load_list(n4, "n4_sb")
+        n5_sb = load_list(n5, "n5_sb")
+        n6_sb = load_list(n6, "n6_sb")
+        ga_sb = load_rows(ga, "ga_sb", nc.gpsimd)
+        tau_sb = load_rows(tau, "tau_sb", nc.gpsimd)
+        tau2_sb = load_rows(tau2, "tau2_sb", nc.gpsimd)
+        gb_sb = load_rows(gb, "gb_sb", nc.gpsimd)
+        tau3_sb = load_rows(tau3, "tau3_sb", nc.gpsimd)
+
+        sig_bias = new([P, PACK], F32, "sig_bias")
+        nc.vector.scalar_tensor_tensor(sig_bias[:], sl_sb[:], -1.0, th_sb[:], ALU.mult, ALU.mult)
+
+        got_bytes = new([P, S + V], U8, "got_bytes")
+        nc.vector.tensor_copy(got_bytes[:, :S], x_bytes[:].indirect(offs_sb[:]))
+        nc.vector.tensor_copy(got_bytes[:, S:], x_bytes[:].indirect(two_sb[:]))
+        x_plane = new([P, S + V], U8, "x_plane")
+        nc.vector.tensor_copy(x_plane[:].bitcast(I32), got_bytes[:].bitcast(I32))
+        for r in range(2):
+            nc.sync.dma_start(out=x_plane[2 + r : P : 32, :].bitcast(I32), in_=got_bytes[16 + r : P : 32, :].bitcast(I32))
+        xa_codes = new([P, S], U32, "xa_codes")
+        nc.vector.tensor_copy(xa_codes[:], x_sb[:].bitcast(U32).indirect(offs_sb[:]))
+        xb_codes = new([P, V], U32, "xb_codes")
+        nc.vector.tensor_copy(xb_codes[:], x_sb[:].bitcast(U32).indirect(two_sb[:]))
+
+        def dealt(tile):
+            return tile[:].rearrange("p (u m j) -> p m j u", u=PACK, j=PACK)
+
+        def by_fours(ap):
+            return ap.rearrange("p j (m u) -> p m j u", u=PACK)
+
+        def quantise(src, width, name, pieces):
+            codes = new([P, width], U32, name + "_codes")
+            plane = new([P, width], U8, name + "_plane")
+            step = width // pieces
+            for i in range(pieces):
+                cols = slice(i * step, (i + 1) * step)
+                nc.vector.quantize_mx(out=codes[:, cols].bitcast(FP8X4), scales=plane[:, cols], in_=src[:, PACK * i * step : PACK * (i + 1) * step])
+            return codes, plane
+
+        w1_bf = new([P, PACK * H], BF16, "w1_bf")
+        nc.scalar.copy(dealt(w1_bf)[:, : P // 2], by_fours(w1_raw[0][:]))
+        nc.vector.tensor_copy(dealt(w1_bf)[:, P // 2 :], by_fours(w1_raw[1][:]))
+        w1_codes, w1_plane = quantise(w1_bf, H, "w1", 2)
+
+        def product(tag, t, lhs_codes, lhs_plane, rhs_codes, rhs_plane, width):
+            acc = psum.tile([P, 512], F32, name=tag, tag=tag)
+            cols = slice(t * P, (t + 1) * P)
+            nc.tensor.matmul_mx(out=acc[:, :width], lhsT=lhs_codes[:, cols].bitcast(FP8X4), lhsT_scale=lhs_plane[:, cols], rhs=rhs_codes.bitcast(FP8X4), rhs_scale=rhs_plane, start=True, stop=True)
+            return acc
+
+        a_ps = [product("bank%d" % t, t, w1_codes, w1_plane, xa_codes[:], x_plane[:, :S], S) for t in range(PACK)]
+        a_sb = [new([P, 2 * S], F32, "a_sb%d" % t) for t in range(PACK)]
+        sg = new([P, PACK, S], F32, "sg")
+        win = [new([P, 2 * S], F32, "win%d" % t) for t in range(PACK)]
+        own = new([P, PACK, S], F32, "own")
+        z = new([P, PACK, S], F32, "z")
+
+        def a_out(t, engine_copy):
+            engine_copy(a_sb[t][:, :S], a_ps[t][:])
+
+        def sigmoid(t):
+            nc.scalar.activation(sg[:, t, :], a_sb[t][:].indirect(n1_sb[:]), ACT.Sigmoid, bias=sig_bias[:, t : t + 1], scale=sl_sb[:, t : t + 1])
+
+        def gate(t):
+            nc.vector.scalar_tensor_tensor(own[:, t, :], a_ps[t][:], ga_sb[:, t : t + 1], sg[:, t, :], ALU.mult, ALU.mult)
+
+        def double(t):
+            nc.vector.tensor_scalar(win[t][:, :S], own[:, t, :], -0.5, None, ALU.mult)
+
+        def neighbours(t):
+            nc.vector.tensor_tensor(z[:, t, :], win[t][:].indirect(n2_sb[:]), own[:, t, :], ALU.add)
+
+        a_out(0, nc.vector.tensor_copy)
+        sigmoid(0)
+        a_out(1, nc.scalar.copy)
+        sigmoid(1)
+        a_out(2, nc.scalar.copy)
+        sigmoid(2)
+        a_out(3, nc.scalar.copy)
+        sigmoid(3)
+
+        w2_bf = new([P, PACK * H], BF16, "w2_bf")
+        nc.vector.tensor_copy(dealt(w2_bf), by_fours(w2_raw[:]))
+        gate(0)
+        w2_codes, w2_plane = quantise(w2_bf, H, "w2", 1)
+        double(0)
+        gate(1)
+        b_ps = [product("bank%d" % (PACK + t), t, w2_codes, w2_plane, xb_codes[:], x_plane[:, S:], V) for t in range(PACK)]
+        b_sb = [new([P, 2 * V], F32, "b_sb%d" % t) for t in range(PACK)]
+        top = new([P, PACK], F32, "top")
+        b_bias = new([P, 2, PACK], F32, "b_bias")
+        for t in range(PACK):
+            nc.vector.tensor_scalar(b_sb[t][:, :V], b_ps[t][:, :V], 1.0, None, ALU.mult, ALU.max, accum_out=top[:, t : t + 1])
+        double(1)
+        for e, rate in enumerate((tau_sb, tau2_sb)):
+            nc.vector.scalar_tensor_tensor(b_bias[:, e, :], rate[:], -1.0, top[:], ALU.mult, ALU.mult)
+        ea = new([P, PACK, 2, V], F32, "ea")
+        for t in range(PACK):
+            nc.scalar.activation(ea[:, t, 0, :], b_sb[t][:].indirect(n3_sb[:]), ACT.Exp, bias=b_bias[:, 0, t : t + 1], scale=tau_sb[:, t : t + 1])
+            nc.scalar.activation(ea[:, t, 1, :], b_sb[t][:].indirect(n4_sb[:]), ACT.Exp, bias=b_bias[:, 1, t : t + 1], scale=tau2_sb[:, t : t + 1])
+
+        neighbours(0)
+        gate(2)
+        neighbours(1)
+        double(2)
+        gate(3)
+        neighbours(2)
+        double(3)
+        eb = new([P, 2, PACK, V], F32, "eb")
+
+        def weigh(t):
+            nc.vector.tensor_scalar(eb[:, :, t, :], ea[:, t, :, :], gb_sb[:, t : t + 1], 3.0, ALU.mult, ALU.mult)
+
+        weigh(0)
+        neighbours(3)
+        weigh(1)
+        z_bf = new([P, PACK * S], BF16, "z_bf")
+        nc.vector.tensor_copy(dealt(z_bf), by_fours(z[:]))
+        weigh(2)
+        z_codes, z_plane = quantise(z_bf, S, "z", 1)
+        weigh(3)
+        z2_bf = new([P, PACK * V], BF16, "z2_bf")
+        nc.vector.tensor_tensor(
+            z2_bf[:].rearrange("p (c i t) -> p c t i", i=4, t=PACK),
+            eb[:, 0].rearrange("p t (c i) -> p c t i", i=4),
+            eb[:, 1].rearrange("p t (c i) -> p c t i", i=4),
+            ALU.subtract,
+        )
+        z2_codes, z2_plane = quantise(z2_bf, V, "z2", 1)
+
+        s_ps = [product("bank%d" % t, t, z_codes, z_plane, z2_codes[:], z2_plane[:], V) for t in range(PACK)]
+        s_sb = [new([P, (PACK if t == PACK - 1 else 2) * V], F32, "s_sb%d" % t) for t in range(PACK)]
+        top2 = new([P, PACK], F32, "top2")
+        s_bias = new([P, PACK], F32, "s_bias")
+        es = new([P, PACK, 2, V], F32, "es")
+        total = new([P, PACK, V], F32, "total")
+        last_logs = new([P, V], F32, "last_logs")
+        logs = [s_sb[PACK - 1][:, (t + 1) * V : (t + 2) * V] for t in range(PACK - 1)] + [last_logs[:]]
+        res = new([P, PACK, V], F32, "res")
+        for t in range(PACK):
+            nc.vector.tensor_scalar(s_sb[t][:, :V], s_ps[t][:, :V], 0.0625, None, ALU.mult, ALU.max, accum_out=top2[:, t : t + 1])
+            nc.vector.tensor_scalar(s_bias[:, t : t + 1], tau3_sb[:, t : t + 1], top2[:, t : t + 1], -1.0, ALU.mult, ALU.mult)
+        for t in range(PACK):
+            nc.scalar.activation(es[:, t, 0, :], s_sb[t][:].indirect(n5_sb[:]), ACT.Exp, bias=s_bias[:, t : t + 1], scale=tau3_sb[:, t : t + 1])
+            nc.scalar.activation(es[:, t, 1, :], s_sb[t][:].indirect(n6_sb[:]), ACT.Exp, bias=s_bias[:, t : t + 1], scale=tau3_sb[:, t : t + 1])
+            nc.vector.scalar_tensor_tensor(total[:, t, :], es[:, t, 0, :], 0.25, es[:, t, 1, :], ALU.add, ALU.add)
+        out_rows = out.rearrange("(p t) v -> p t v", t=PACK)
+        for t in range(PACK):
+            nc.scalar.activation(logs[t], total[:, t, :], ACT.Ln)
+            nc.vector.tensor_tensor(res[:, t, :], logs[t], s_sb[t][:, :V], ALU.add)
+            nc.sync.dma_start(out=out_rows[:, t, :], in_=res[:, t, :])

@@ -17,6 +17,7 @@ ACT = mybir.ActivationFunctionType
 
 P = 128
 PACK = 4
+Z_SPLIT = 104
 
 
 def tile_picked_hkqehpetwelg_none_p_kernel(tc, x_words, x_scales, w1, w2, sl, th, tau, tau2, ga, gb, tau3, offs, two, n1, n2, n3, n4, n5, n6, out):
@@ -38,37 +39,33 @@ def tile_picked_hkqehpetwelg_none_p_kernel(tc, x_words, x_scales, w1, w2, sl, th
             queue.dma_start(out=t[:], in_=src.rearrange("(p t) o -> p (t o)", t=PACK))
             return t
 
+        warm_in = new([P, 1], F32, "warm_in")
+        nc.gpsimd.memset(warm_in[:], 0.0)
+        warm_out = new([P, 1], F32, "warm_out")
+        nc.scalar.activation(warm_out[:], warm_in[:], ACT.Sigmoid)
         x_bytes = new([P, T], U8, "x_bytes")
         nc.vector.memset(x_bytes[:].bitcast(I32), 0)
         offs_sb = load_list(offs, "offs_sb")
+        two_sb = load_list(two, "two_sb")
         scale_rows = x_scales[0].rearrange("(g r) c -> r g c", r=2)
         for r in range(2):
-            nc.scalar.dma_start(out=x_bytes[r:P:16, :].bitcast(I32), in_=scale_rows[r].bitcast(I32))
-        two_sb = load_list(two, "two_sb")
+            nc.sync.dma_start(out=x_bytes[r:P:16, :].bitcast(I32), in_=scale_rows[r].bitcast(I32))
         x_sb = new([P, T], I32, "x_sb")
         nc.sync.dma_start(out=x_sb[:], in_=x_words[0].rearrange("p c r -> p (c r)").bitcast(I32))
-        sl_sb = load_rows(sl, "sl_sb", nc.sync)
-        th_sb = load_rows(th, "th_sb", nc.sync)
-        n1_sb = load_list(n1, "n1_sb")
-        n2_sb = load_list(n2, "n2_sb")
-        n3_sb = load_list(n3, "n3_sb")
         HALF = H // 2
         w1_raw = [new([P, PACK, HALF], F32, "w1_raw%d" % h) for h in range(2)]
         for h in range(2):
             nc.sync.dma_start(out=w1_raw[h][:], in_=w1.rearrange("(p j) c -> p j c", j=PACK)[:, :, h * HALF : (h + 1) * HALF])
-        w2_raw = new([P, PACK, H], F32, "w2_raw")
-        nc.sync.dma_start(out=w2_raw[:], in_=w2.rearrange("(p j) c -> p j c", j=PACK))
-        n4_sb = load_list(n4, "n4_sb")
-        n5_sb = load_list(n5, "n5_sb")
-        n6_sb = load_list(n6, "n6_sb")
-        ga_sb = load_rows(ga, "ga_sb", nc.gpsimd)
-        tau_sb = load_rows(tau, "tau_sb", nc.gpsimd)
-        tau2_sb = load_rows(tau2, "tau2_sb", nc.gpsimd)
-        gb_sb = load_rows(gb, "gb_sb", nc.gpsimd)
-        tau3_sb = load_rows(tau3, "tau3_sb", nc.gpsimd)
+        n1_sb = load_list(n1, "n1_sb")
+        n2_sb = load_list(n2, "n2_sb")
+        n3_sb = load_list(n3, "n3_sb")
+        sl_sb = load_rows(sl, "sl_sb", nc.gpsimd)
+        th_sb = load_rows(th, "th_sb", nc.gpsimd)
 
+        slth = new([P, PACK], F32, "slth")
+        nc.gpsimd.tensor_tensor(slth[:], sl_sb[:], th_sb[:], ALU.mult)
         sig_bias = new([P, PACK], F32, "sig_bias")
-        nc.vector.scalar_tensor_tensor(sig_bias[:], sl_sb[:], -1.0, th_sb[:], ALU.mult, ALU.mult)
+        nc.gpsimd.tensor_scalar(sig_bias[:], slth[:], -1.0, 0.0, ALU.mult, ALU.add)
 
         got_bytes = new([P, S + V], U8, "got_bytes")
         nc.vector.tensor_copy(got_bytes[:, :S], x_bytes[:].indirect(offs_sb[:]))
@@ -77,6 +74,16 @@ def tile_picked_hkqehpetwelg_none_p_kernel(tc, x_words, x_scales, w1, w2, sl, th
         nc.vector.tensor_copy(x_plane[:].bitcast(I32), got_bytes[:].bitcast(I32))
         for r in range(2):
             nc.sync.dma_start(out=x_plane[2 + r : P : 32, :].bitcast(I32), in_=got_bytes[16 + r : P : 32, :].bitcast(I32))
+        w2_raw = new([P, PACK, H], F32, "w2_raw")
+        nc.sync.dma_start(out=w2_raw[:], in_=w2.rearrange("(p j) c -> p j c", j=PACK))
+        n4_sb = load_list(n4, "n4_sb")
+        tau_sb = load_rows(tau, "tau_sb", nc.sync)
+        tau2_sb = load_rows(tau2, "tau2_sb", nc.sync)
+        gb_sb = load_rows(gb, "gb_sb", nc.sync)
+        ga_sb = load_rows(ga, "ga_sb", nc.sync)
+        n5_sb = load_list(n5, "n5_sb")
+        n6_sb = load_list(n6, "n6_sb")
+        tau3_sb = load_rows(tau3, "tau3_sb", nc.sync)
         xa_codes = new([P, S], U32, "xa_codes")
         nc.vector.tensor_copy(xa_codes[:], x_sb[:].bitcast(U32).indirect(offs_sb[:]))
         xb_codes = new([P, V], U32, "xb_codes")
@@ -99,8 +106,9 @@ def tile_picked_hkqehpetwelg_none_p_kernel(tc, x_words, x_scales, w1, w2, sl, th
 
         w1_bf = new([P, PACK * H], BF16, "w1_bf")
         nc.scalar.copy(dealt(w1_bf)[:, : P // 2], by_fours(w1_raw[0][:]))
-        nc.vector.tensor_copy(dealt(w1_bf)[:, P // 2 :], by_fours(w1_raw[1][:]))
-        w1_codes, w1_plane = quantise(w1_bf, H, "w1", 2)
+        nc.vector.tensor_copy(dealt(w1_bf)[:, P // 2 : Z_SPLIT], by_fours(w1_raw[1][:])[:, : Z_SPLIT - P // 2])
+        nc.scalar.copy(dealt(w1_bf)[:, Z_SPLIT:], by_fours(w1_raw[1][:])[:, Z_SPLIT - P // 2 :])
+        w1_codes, w1_plane = quantise(w1_bf, H, "w1", PACK)
 
         def product(tag, t, lhs_codes, lhs_plane, rhs_codes, rhs_plane, width):
             acc = psum.tile([P, 512], F32, name=tag, tag=tag)
@@ -109,13 +117,14 @@ def tile_picked_hkqehpetwelg_none_p_kernel(tc, x_words, x_scales, w1, w2, sl, th
             return acc
 
         a_ps = [product("bank%d" % t, t, w1_codes, w1_plane, xa_codes[:], x_plane[:, :S], S) for t in range(PACK)]
-        a_sb = [new([P, 2 * S], F32, "a_sb%d" % t) for t in range(PACK)]
+        a_sb = {}
         sg = new([P, PACK, S], F32, "sg")
         win = [new([P, 2 * S], F32, "win%d" % t) for t in range(PACK)]
         own = new([P, PACK, S], F32, "own")
         z = new([P, PACK, S], F32, "z")
 
         def a_out(t, engine_copy):
+            a_sb[t] = new([P, 2 * S], F32, "a_sb%d" % t)
             engine_copy(a_sb[t][:, :S], a_ps[t][:])
 
         def sigmoid(t):
@@ -124,6 +133,15 @@ def tile_picked_hkqehpetwelg_none_p_kernel(tc, x_words, x_scales, w1, w2, sl, th
         def gate(t):
             nc.vector.scalar_tensor_tensor(own[:, t, :], a_ps[t][:], ga_sb[:, t : t + 1], sg[:, t, :], ALU.mult, ALU.mult)
 
+        def gate_window(t):
+            nc.vector.scalar_tensor_tensor(win[t][:, :S], a_ps[t][:], ga_sb[:, t : t + 1], sg[:, t, :], ALU.mult, ALU.mult)
+
+        def fetch(t):
+            nc.scalar.activation(own[:, t, :], win[t][:].indirect(n2_sb[:]), ACT.Copy, scale=-0.5)
+
+        def join(t):
+            nc.vector.tensor_tensor(z[:, t, :], win[t][:, :S], own[:, t, :], ALU.add)
+
         def double(t):
             nc.vector.tensor_scalar(win[t][:, :S], own[:, t, :], -0.5, None, ALU.mult)
 
@@ -131,64 +149,83 @@ def tile_picked_hkqehpetwelg_none_p_kernel(tc, x_words, x_scales, w1, w2, sl, th
             nc.vector.tensor_tensor(z[:, t, :], win[t][:].indirect(n2_sb[:]), own[:, t, :], ALU.add)
 
         a_out(0, nc.vector.tensor_copy)
+        a_out(1, nc.vector.tensor_copy)
+        a_out(2, nc.vector.tensor_copy)
         sigmoid(0)
-        a_out(1, nc.scalar.copy)
-        sigmoid(1)
-        a_out(2, nc.scalar.copy)
-        sigmoid(2)
         a_out(3, nc.scalar.copy)
-        sigmoid(3)
-
+        for t in range(1, PACK):
+            sigmoid(t)
         w2_bf = new([P, PACK * H], BF16, "w2_bf")
         nc.vector.tensor_copy(dealt(w2_bf), by_fours(w2_raw[:]))
-        gate(0)
         w2_codes, w2_plane = quantise(w2_bf, H, "w2", 1)
-        double(0)
-        gate(1)
+        gate_window(0)
+        fetch(0)
         b_ps = [product("bank%d" % (PACK + t), t, w2_codes, w2_plane, xb_codes[:], x_plane[:, S:], V) for t in range(PACK)]
         b_sb = [new([P, 2 * V], F32, "b_sb%d" % t) for t in range(PACK)]
         top = new([P, PACK], F32, "top")
         b_bias = new([P, 2, PACK], F32, "b_bias")
         for t in range(PACK):
             nc.vector.tensor_scalar(b_sb[t][:, :V], b_ps[t][:, :V], 1.0, None, ALU.mult, ALU.max, accum_out=top[:, t : t + 1])
-        double(1)
+        gate(1)
         for e, rate in enumerate((tau_sb, tau2_sb)):
             nc.vector.scalar_tensor_tensor(b_bias[:, e, :], rate[:], -1.0, top[:], ALU.mult, ALU.mult)
         ea = new([P, PACK, 2, V], F32, "ea")
-        for t in range(PACK):
-            nc.scalar.activation(ea[:, t, 0, :], b_sb[t][:].indirect(n3_sb[:]), ACT.Exp, bias=b_bias[:, 0, t : t + 1], scale=tau_sb[:, t : t + 1])
-            nc.scalar.activation(ea[:, t, 1, :], b_sb[t][:].indirect(n4_sb[:]), ACT.Exp, bias=b_bias[:, 1, t : t + 1], scale=tau2_sb[:, t : t + 1])
-
-        neighbours(0)
-        gate(2)
-        neighbours(1)
-        double(2)
-        gate(3)
-        neighbours(2)
-        double(3)
         eb = new([P, 2, PACK, V], F32, "eb")
-
-        def weigh(t):
-            nc.vector.tensor_scalar(eb[:, :, t, :], ea[:, t, :, :], gb_sb[:, t : t + 1], 3.0, ALU.mult, ALU.mult)
-
-        weigh(0)
-        neighbours(3)
-        weigh(1)
-        z_bf = new([P, PACK * S], BF16, "z_bf")
-        nc.vector.tensor_copy(dealt(z_bf), by_fours(z[:]))
-        weigh(2)
-        z_codes, z_plane = quantise(z_bf, S, "z", 1)
-        weigh(3)
         z2_bf = new([P, PACK * V], BF16, "z2_bf")
-        nc.vector.tensor_tensor(
-            z2_bf[:].rearrange("p (c i t) -> p c t i", i=4, t=PACK),
-            eb[:, 0].rearrange("p t (c i) -> p c t i", i=4),
-            eb[:, 1].rearrange("p t (c i) -> p c t i", i=4),
-            ALU.subtract,
-        )
-        z2_codes, z2_plane = quantise(z2_bf, V, "z2", 1)
+        z2_codes = new([P, V], U32, "z2_codes")
+        z2_plane = new([P, V], U8, "z2_plane")
 
-        s_ps = [product("bank%d" % t, t, z_codes, z_plane, z2_codes[:], z2_plane[:], V) for t in range(PACK)]
+        def exps(t, cols):
+            offsets = slice(cols.start // 16, cols.stop // 16)
+            for e, (places, rate) in enumerate(((n3_sb, tau_sb), (n4_sb, tau2_sb))):
+                nc.scalar.activation(ea[:, t, e, cols], b_sb[t][:].indirect(places[:, offsets]), ACT.Exp, bias=b_bias[:, e, t : t + 1], scale=rate[:, t : t + 1])
+
+        def weigh(t, cols):
+            nc.vector.tensor_scalar(eb[:, :, t, cols], ea[:, t, :, cols], gb_sb[:, t : t + 1], 3.0, ALU.mult, ALU.mult)
+
+        def differ(cols):
+            nc.vector.tensor_tensor(
+                z2_bf[:, PACK * cols.start : PACK * cols.stop].rearrange("p (c i t) -> p c t i", i=4, t=PACK),
+                eb[:, 0, :, cols].rearrange("p t (c i) -> p c t i", i=4),
+                eb[:, 1, :, cols].rearrange("p t (c i) -> p c t i", i=4),
+                ALU.subtract,
+            )
+
+        def quantise_z2(cols):
+            nc.vector.quantize_mx(out=z2_codes[:, cols].bitcast(FP8X4), scales=z2_plane[:, cols], in_=z2_bf[:, PACK * cols.start : PACK * cols.stop])
+
+        whole, low, high = slice(0, V), slice(0, V // 2), slice(V // 2, V)
+        for t in range(PACK - 1):
+            exps(t, whole)
+        exps(PACK - 1, low)
+        exps(PACK - 1, high)
+        for t in range(1, PACK - 1):
+            double(t)
+            gate(t + 1)
+            neighbours(t)
+        double(PACK - 1)
+        join(0)
+        neighbours(PACK - 1)
+        z_bf = new([P, PACK * S], BF16, "z_bf")
+        z_codes = new([P, S], U32, "z_codes")
+        z_plane = new([P, S], U8, "z_plane")
+
+        def quantise_z(h):
+            cols = slice(h * 256, (h + 1) * 256)
+            nc.vector.quantize_mx(out=z_codes[:, cols].bitcast(FP8X4), scales=z_plane[:, cols], in_=z_bf[:, PACK * cols.start : PACK * cols.stop])
+
+        for h in range(2):
+            nc.scalar.copy(dealt(z_bf)[:, :, :, 2 * h : 2 * h + 2], by_fours(z[:])[:, :, :, 2 * h : 2 * h + 2])
+        for t in range(PACK - 1):
+            weigh(t, whole)
+        weigh(3, low)
+        differ(low)
+        weigh(3, high)
+        quantise_z2(low)
+        differ(high)
+        quantise_z(0)
+        quantise_z2(high)
+
         s_sb = [new([P, (PACK if t == PACK - 1 else 2) * V], F32, "s_sb%d" % t) for t in range(PACK)]
         top2 = new([P, PACK], F32, "top2")
         s_bias = new([P, PACK], F32, "s_bias")
@@ -198,14 +235,18 @@ def tile_picked_hkqehpetwelg_none_p_kernel(tc, x_words, x_scales, w1, w2, sl, th
         logs = [s_sb[PACK - 1][:, (t + 1) * V : (t + 2) * V] for t in range(PACK - 1)] + [last_logs[:]]
         res = new([P, PACK, V], F32, "res")
         for t in range(PACK):
-            nc.vector.tensor_scalar(s_sb[t][:, :V], s_ps[t][:, :V], 0.0625, None, ALU.mult, ALU.max, accum_out=top2[:, t : t + 1])
+            if t == 2:
+                quantise_z(1)
+            s_ps = product("bank%d" % t, t, z_codes, z_plane, z2_codes[:], z2_plane[:], V)
+            nc.vector.tensor_scalar(s_sb[t][:, :V], s_ps[:, :V], 0.0625, None, ALU.mult, ALU.max, accum_out=top2[:, t : t + 1])
             nc.vector.tensor_scalar(s_bias[:, t : t + 1], tau3_sb[:, t : t + 1], top2[:, t : t + 1], -1.0, ALU.mult, ALU.mult)
         for t in range(PACK):
             nc.scalar.activation(es[:, t, 0, :], s_sb[t][:].indirect(n5_sb[:]), ACT.Exp, bias=s_bias[:, t : t + 1], scale=tau3_sb[:, t : t + 1])
             nc.scalar.activation(es[:, t, 1, :], s_sb[t][:].indirect(n6_sb[:]), ACT.Exp, bias=s_bias[:, t : t + 1], scale=tau3_sb[:, t : t + 1])
             nc.vector.scalar_tensor_tensor(total[:, t, :], es[:, t, 0, :], 0.25, es[:, t, 1, :], ALU.add, ALU.add)
         out_rows = out.rearrange("(p t) v -> p t v", t=PACK)
-        for t in range(PACK):
-            nc.scalar.activation(logs[t], total[:, t, :], ACT.Ln)
-            nc.vector.tensor_tensor(res[:, t, :], logs[t], s_sb[t][:, :V], ALU.add)
-            nc.sync.dma_start(out=out_rows[:, t, :], in_=res[:, t, :])
+        pieces = [(t, whole) for t in range(PACK)]
+        for t, cols in pieces:
+            nc.scalar.activation(logs[t][:, cols], total[:, t, cols], ACT.Ln)
+            nc.vector.tensor_tensor(res[:, t, cols], logs[t][:, cols], s_sb[t][:, cols], ALU.add)
+            nc.sync.dma_start(out=out_rows[:, t, cols], in_=res[:, t, cols])

from contextlib import ExitStack

import concourse.mybir as mybir

K, T, S, V, H = 512, 2048, 512, 256, 512
FLOPS = 2 * K * H * S + 2 * K * H * V + 2 * H * S * V

F32 = mybir.dt.float32
BF16 = mybir.dt.bfloat16
I32 = mybir.dt.int32
U32 = mybir.dt.uint32
U16 = mybir.dt.uint16
U8 = mybir.dt.uint8
FP8X4 = mybir.dt.float8_e4m3fn_x4
ALU = mybir.AluOpType
ACT = mybir.ActivationFunctionType

P = 128
PACK = 4
Z_SPLIT = 104


def tile_picked_hkqehpetwelg_none_p_kernel(tc, x_words, x_scales, w1, w2, sl, th, tau, tau2, ga, gb, tau3, offs, two, n1, n2, n3, n4, n5, n6, out):
    nc = tc.nc
    with ExitStack() as ctx:
        keep = ctx.enter_context(tc.tile_pool(name="keep", bufs=1))
        psum = ctx.enter_context(tc.psum_pool(name="psum", bufs=1))

        def new(shape, dtype, name):
            return keep.tile(shape, dtype, name=name, align_bytes=64)

        def load_list(src, name):
            t = new(list(src.shape), U16, name)
            nc.sync.dma_start(t[:], src)
            return t

        def load_rows(src, name, queue):
            t = new([P, PACK], F32, name)
            queue.dma_start(out=t[:], in_=src.rearrange("(p t) o -> p (t o)", t=PACK))
            return t

        warm_in = new([P, 1], F32, "warm_in")
        nc.gpsimd.memset(warm_in[:], 0.0)
        warm_out = new([P, 1], F32, "warm_out")
        nc.scalar.activation(warm_out[:], warm_in[:], ACT.Sigmoid)
        x_bytes = new([P, T], U8, "x_bytes")
        nc.vector.memset(x_bytes[:].bitcast(I32), 0)
        offs_sb = load_list(offs, "offs_sb")
        two_sb = load_list(two, "two_sb")
        scale_rows = x_scales[0].rearrange("(g r) c -> r g c", r=2)
        for r in range(2):
            nc.sync.dma_start(out=x_bytes[r:P:16, :].bitcast(I32), in_=scale_rows[r].bitcast(I32))
        x_sb = new([P, T], I32, "x_sb")
        nc.sync.dma_start(out=x_sb[:], in_=x_words[0].rearrange("p c r -> p (c r)").bitcast(I32))
        HALF = H // 2
        w1_raw = [new([P, PACK, HALF], F32, "w1_raw%d" % h) for h in range(2)]
        for h in range(2):
            nc.sync.dma_start(out=w1_raw[h][:], in_=w1.rearrange("(p j) c -> p j c", j=PACK)[:, :, h * HALF : (h + 1) * HALF])
        n1_sb = load_list(n1, "n1_sb")
        n2_sb = load_list(n2, "n2_sb")
        n3_sb = load_list(n3, "n3_sb")
        sl_sb = load_rows(sl, "sl_sb", nc.gpsimd)
        th_sb = load_rows(th, "th_sb", nc.gpsimd)

        slth = new([P, PACK], F32, "slth")
        nc.gpsimd.tensor_tensor(slth[:], sl_sb[:], th_sb[:], ALU.mult)
        sig_bias = new([P, PACK], F32, "sig_bias")
        nc.gpsimd.tensor_scalar(sig_bias[:], slth[:], -1.0, 0.0, ALU.mult, ALU.add)

        got_bytes = new([P, S + V], U8, "got_bytes")
        nc.vector.tensor_copy(got_bytes[:, :S], x_bytes[:].indirect(offs_sb[:]))
        nc.vector.tensor_copy(got_bytes[:, S:], x_bytes[:].indirect(two_sb[:]))
        x_plane = new([P, S + V], U8, "x_plane")
        nc.vector.tensor_copy(x_plane[:].bitcast(I32), got_bytes[:].bitcast(I32))
        for r in range(2):
            nc.sync.dma_start(out=x_plane[2 + r : P : 32, :].bitcast(I32), in_=got_bytes[16 + r : P : 32, :].bitcast(I32))
        w2_raw = new([P, PACK, H], F32, "w2_raw")
        nc.sync.dma_start(out=w2_raw[:], in_=w2.rearrange("(p j) c -> p j c", j=PACK))
        n4_sb = load_list(n4, "n4_sb")
        tau_sb = load_rows(tau, "tau_sb", nc.sync)
        tau2_sb = load_rows(tau2, "tau2_sb", nc.sync)
        gb_sb = load_rows(gb, "gb_sb", nc.sync)
        ga_sb = load_rows(ga, "ga_sb", nc.sync)
        n5_sb = load_list(n5, "n5_sb")
        n6_sb = load_list(n6, "n6_sb")
        tau3_sb = load_rows(tau3, "tau3_sb", nc.sync)
        xa_codes = new([P, S], U32, "xa_codes")
        nc.vector.tensor_copy(xa_codes[:], x_sb[:].bitcast(U32).indirect(offs_sb[:]))
        xb_codes = new([P, V], U32, "xb_codes")
        nc.vector.tensor_copy(xb_codes[:], x_sb[:].bitcast(U32).indirect(two_sb[:]))

        def dealt(tile):
            return tile[:].rearrange("p (u m j) -> p m j u", u=PACK, j=PACK)

        def by_fours(ap):
            return ap.rearrange("p j (m u) -> p m j u", u=PACK)

        def quantise(src, width, name, pieces):
            codes = new([P, width], U32, name + "_codes")
            plane = new([P, width], U8, name + "_plane")
            step = width // pieces
            for i in range(pieces):
                cols = slice(i * step, (i + 1) * step)
                nc.vector.quantize_mx(out=codes[:, cols].bitcast(FP8X4), scales=plane[:, cols], in_=src[:, PACK * i * step : PACK * (i + 1) * step])
            return codes, plane

        w1_bf = new([P, PACK * H], BF16, "w1_bf")
        nc.scalar.copy(dealt(w1_bf)[:, : P // 2], by_fours(w1_raw[0][:]))
        nc.vector.tensor_copy(dealt(w1_bf)[:, P // 2 : Z_SPLIT], by_fours(w1_raw[1][:])[:, : Z_SPLIT - P // 2])
        nc.scalar.copy(dealt(w1_bf)[:, Z_SPLIT:], by_fours(w1_raw[1][:])[:, Z_SPLIT - P // 2 :])
        w1_codes, w1_plane = quantise(w1_bf, H, "w1", PACK)

        def product(tag, t, lhs_codes, lhs_plane, rhs_codes, rhs_plane, width):
            acc = psum.tile([P, 512], F32, name=tag, tag=tag)
            cols = slice(t * P, (t + 1) * P)
            nc.tensor.matmul_mx(out=acc[:, :width], lhsT=lhs_codes[:, cols].bitcast(FP8X4), lhsT_scale=lhs_plane[:, cols], rhs=rhs_codes.bitcast(FP8X4), rhs_scale=rhs_plane, start=True, stop=True)
            return acc

        a_ps = [product("bank%d" % t, t, w1_codes, w1_plane, xa_codes[:], x_plane[:, :S], S) for t in range(PACK)]
        a_sb = {}
        sg = new([P, PACK, S], F32, "sg")
        win = [new([P, 2 * S], F32, "win%d" % t) for t in range(PACK)]
        own = new([P, PACK, S], F32, "own")
        z = new([P, PACK, S], F32, "z")

        def a_out(t, engine_copy):
            a_sb[t] = new([P, 2 * S], F32, "a_sb%d" % t)
            engine_copy(a_sb[t][:, :S], a_ps[t][:])

        def sigmoid(t):
            nc.scalar.activation(sg[:, t, :], a_sb[t][:].indirect(n1_sb[:]), ACT.Sigmoid, bias=sig_bias[:, t : t + 1], scale=sl_sb[:, t : t + 1])

        def gate(t):
            nc.vector.scalar_tensor_tensor(own[:, t, :], a_ps[t][:], ga_sb[:, t : t + 1], sg[:, t, :], ALU.mult, ALU.mult)

        def gate_window(t):
            nc.vector.scalar_tensor_tensor(win[t][:, :S], a_ps[t][:], ga_sb[:, t : t + 1], sg[:, t, :], ALU.mult, ALU.mult)

        def fetch(t):
            nc.scalar.activation(own[:, t, :], win[t][:].indirect(n2_sb[:]), ACT.Copy, scale=-0.5)

        def join(t):
            nc.vector.tensor_tensor(z[:, t, :], win[t][:, :S], own[:, t, :], ALU.add)

        def double(t):
            nc.vector.tensor_scalar(win[t][:, :S], own[:, t, :], -0.5, None, ALU.mult)

        def neighbours(t):
            nc.vector.tensor_tensor(z[:, t, :], win[t][:].indirect(n2_sb[:]), own[:, t, :], ALU.add)

        a_out(0, nc.vector.tensor_copy)
        a_out(1, nc.vector.tensor_copy)
        a_out(2, nc.vector.tensor_copy)
        sigmoid(0)
        a_out(3, nc.scalar.copy)
        for t in range(1, PACK):
            sigmoid(t)
        w2_bf = new([P, PACK * H], BF16, "w2_bf")
        nc.vector.tensor_copy(dealt(w2_bf), by_fours(w2_raw[:]))
        w2_codes, w2_plane = quantise(w2_bf, H, "w2", 1)
        gate_window(0)
        fetch(0)
        b_ps = [product("bank%d" % (PACK + t), t, w2_codes, w2_plane, xb_codes[:], x_plane[:, S:], V) for t in range(PACK)]
        b_sb = [new([P, 2 * V], F32, "b_sb%d" % t) for t in range(PACK)]
        top = new([P, PACK], F32, "top")
        b_bias = new([P, 2, PACK], F32, "b_bias")
        for t in range(PACK):
            nc.vector.tensor_scalar(b_sb[t][:, :V], b_ps[t][:, :V], 1.0, None, ALU.mult, ALU.max, accum_out=top[:, t : t + 1])
        gate(1)
        for e, rate in enumerate((tau_sb, tau2_sb)):
            nc.vector.scalar_tensor_tensor(b_bias[:, e, :], rate[:], -1.0, top[:], ALU.mult, ALU.mult)
        ea = new([P, PACK, 2, V], F32, "ea")
        eb = new([P, 2, PACK, V], F32, "eb")
        z2_bf = new([P, PACK * V], BF16, "z2_bf")
        z2_codes = new([P, V], U32, "z2_codes")
        z2_plane = new([P, V], U8, "z2_plane")

        def exps(t, cols):
            offsets = slice(cols.start // 16, cols.stop // 16)
            for e, (places, rate) in enumerate(((n3_sb, tau_sb), (n4_sb, tau2_sb))):
                nc.scalar.activation(ea[:, t, e, cols], b_sb[t][:].indirect(places[:, offsets]), ACT.Exp, bias=b_bias[:, e, t : t + 1], scale=rate[:, t : t + 1])

        def weigh(t, cols):
            nc.vector.tensor_scalar(eb[:, :, t, cols], ea[:, t, :, cols], gb_sb[:, t : t + 1], 3.0, ALU.mult, ALU.mult)

        def differ(cols):
            nc.vector.tensor_tensor(
                z2_bf[:, PACK * cols.start : PACK * cols.stop].rearrange("p (c i t) -> p c t i", i=4, t=PACK),
                eb[:, 0, :, cols].rearrange("p t (c i) -> p c t i", i=4),
                eb[:, 1, :, cols].rearrange("p t (c i) -> p c t i", i=4),
                ALU.subtract,
            )

        def quantise_z2(cols):
            nc.vector.quantize_mx(out=z2_codes[:, cols].bitcast(FP8X4), scales=z2_plane[:, cols], in_=z2_bf[:, PACK * cols.start : PACK * cols.stop])

        whole, low, high = slice(0, V), slice(0, V // 2), slice(V // 2, V)
        for t in range(PACK - 1):
            exps(t, whole)
        exps(PACK - 1, low)
        exps(PACK - 1, high)
        for t in range(1, PACK - 1):
            double(t)
            gate(t + 1)
            neighbours(t)
        double(PACK - 1)
        join(0)
        neighbours(PACK - 1)
        z_bf = new([P, PACK * S], BF16, "z_bf")
        z_codes = new([P, S], U32, "z_codes")
        z_plane = new([P, S], U8, "z_plane")

        def quantise_z(h):
            cols = slice(h * 256, (h + 1) * 256)
            nc.vector.quantize_mx(out=z_codes[:, cols].bitcast(FP8X4), scales=z_plane[:, cols], in_=z_bf[:, PACK * cols.start : PACK * cols.stop])

        for h in range(2):
            nc.scalar.copy(dealt(z_bf)[:, :, :, 2 * h : 2 * h + 2], by_fours(z[:])[:, :, :, 2 * h : 2 * h + 2])
        for t in range(PACK - 1):
            weigh(t, whole)
        weigh(3, low)
        differ(low)
        weigh(3, high)
        quantise_z2(low)
        differ(high)
        quantise_z(0)
        quantise_z2(high)

        s_sb = [new([P, (PACK if t == PACK - 1 else 2) * V], F32, "s_sb%d" % t) for t in range(PACK)]
        top2 = new([P, PACK], F32, "top2")
        s_bias = new([P, PACK], F32, "s_bias")
        es = new([P, PACK, 2, V], F32, "es")
        total = new([P, PACK, V], F32, "total")
        last_logs = new([P, V], F32, "last_logs")
        logs = [s_sb[PACK - 1][:, (t + 1) * V : (t + 2) * V] for t in range(PACK - 1)] + [last_logs[:]]
        res = new([P, PACK, V], F32, "res")
        for t in range(PACK):
            if t == 2:
                quantise_z(1)
            s_ps = product("bank%d" % t, t, z_codes, z_plane, z2_codes[:], z2_plane[:], V)
            nc.vector.tensor_scalar(s_sb[t][:, :V], s_ps[:, :V], 0.0625, None, ALU.mult, ALU.max, accum_out=top2[:, t : t + 1])
            nc.vector.tensor_scalar(s_bias[:, t : t + 1], tau3_sb[:, t : t + 1], top2[:, t : t + 1], -1.0, ALU.mult, ALU.mult)
        for t in range(PACK):
            nc.scalar.activation(es[:, t, 0, :], s_sb[t][:].indirect(n5_sb[:]), ACT.Exp, bias=s_bias[:, t : t + 1], scale=tau3_sb[:, t : t + 1])
            nc.scalar.activation(es[:, t, 1, :], s_sb[t][:].indirect(n6_sb[:]), ACT.Exp, bias=s_bias[:, t : t + 1], scale=tau3_sb[:, t : t + 1])
            nc.vector.scalar_tensor_tensor(total[:, t, :], es[:, t, 0, :], 0.25, es[:, t, 1, :], ALU.add, ALU.add)
        out_rows = out.rearrange("(p t) v -> p t v", t=PACK)
        pieces = [(t, whole) for t in range(PACK)]
        for t, cols in pieces:
            nc.scalar.activation(logs[t][:, cols], total[:, t, cols], ACT.Ln)
            nc.vector.tensor_tensor(res[:, t, cols], logs[t][:, cols], s_sb[t][:, cols], ALU.add)
            nc.sync.dma_start(out=out_rows[:, t, cols], in_=res[:, t, cols])
